import numpy as np
import ml_dtypes


def mxq(x, axis, fmt="e4m3"):
    dtype, down = {"e4m3": (ml_dtypes.float8_e4m3fn, 7), "e5m2": (ml_dtypes.float8_e5m2, 14)}[fmt]
    v = np.moveaxis(np.asarray(x, np.float32).astype(ml_dtypes.bfloat16).astype(np.float64), axis, -1)
    blocks = v.reshape(v.shape[:-1] + (-1, 32))
    amax = np.abs(blocks).max(-1, keepdims=True)
    byte = np.maximum(np.where(amax > 0, np.frexp(amax)[1] - 1 + 127, 0) - down, 1)
    scale = np.exp2(byte - 127.0)
    codes = (blocks / scale).astype(np.float32).astype(dtype).astype(np.float64)
    return np.moveaxis((codes * scale).reshape(v.shape), -1, axis)


WIDE = False


def mx_kscale(k):
    if not WIDE:
        return np.ones(k)
    levels = np.array([10, -10, 5, -5, 0])
    if k % 512:
        return np.exp2(np.random.permutation(np.resize(levels, k // 32))).repeat(32)
    a = np.empty((k // 512, 16))
    for p in range(k // 512):
        a[p, :8] = np.random.permutation(np.resize(levels, 8))
        for g in range(8):
            far = levels[np.abs(levels - a[p, g]) >= 10]
            a[p, g + 8] = far[np.random.randint(len(far))]
    return np.exp2(a.ravel()).repeat(32)


def f64(x):
    return np.asarray(x).astype(np.float64)


def striped(idx):
    return np.tile(idx.reshape(-1, 16).T, (8, 1)).astype(np.uint16)


def unstriped(offs):
    return offs[:16].T.reshape(-1).astype(np.int64)


def striped8(idx):
    return np.concatenate([x.reshape(-1, 16).T for x in idx]).astype(np.uint16)


def runs(offs, k):
    lists = np.stack([offs[16 * r : 16 * r + 16].T.reshape(-1) for r in range(8)]).astype(np.int64)
    return lists[np.arange(k) % 512 // 64]


def pack_weight(w):
    k, n = w.shape
    w = f64(np.asarray(w, np.float32).astype(ml_dtypes.bfloat16)).reshape(k // 32, 32, n)
    amax = np.abs(w).max(1)
    byte = np.clip(np.where(amax > 0, np.frexp(amax)[1] - 1 + 127 - 7, 1), 1, 254)
    scaled = (w * np.exp2(127.0 - byte)[:, None, :]).reshape(k, n).astype(np.float32)
    words = np.ascontiguousarray(scaled.reshape(k // 512, 128, 4, n).transpose(0, 1, 3, 2)).astype(ml_dtypes.float8_e4m3fn).view(np.uint8)
    return words, np.ascontiguousarray(byte.astype(np.uint8).reshape(k // 512, 16, n))


def unpack_weight(words, scales):
    g, p, n, _ = words.shape
    vals = np.ascontiguousarray(words).view(ml_dtypes.float8_e4m3fn).astype(np.float64) * np.repeat(np.exp2(scales.astype(np.float64) - 127.0), 8, axis=1)[..., None]
    return vals.transpose(0, 1, 3, 2).reshape(g * 512, n)


E2M1 = np.array([0.0, 0.5, 1.0, 1.5, 2.0, 3.0, 4.0, 6.0, -0.0, -0.5, -1.0, -1.5, -2.0, -3.0, -4.0, -6.0])


def pack_fp4(w):
    k, n = w.shape
    w = f64(np.asarray(w, np.float32).astype(ml_dtypes.bfloat16)).reshape(k // 32, 32, n)
    amax = np.abs(w).max(1)
    mant, ex = np.frexp(amax / 6.0)
    byte = np.clip(np.where(amax > 0, np.where(mant > 0.5, ex, ex - 1) + 127, 1), 1, 254)
    scaled = (w * np.exp2(127.0 - byte)[:, None, :]).reshape(k, n).astype(np.float32)
    c = np.ascontiguousarray(scaled.reshape(k // 512, 128, 4, n).transpose(0, 1, 3, 2)).astype(ml_dtypes.float4_e2m1fn).view(np.uint8) & 0xF
    words = (c[..., 0::2] | (c[..., 1::2] << 4)).reshape(k // 512, 128, 2 * n)
    return np.ascontiguousarray(words), np.ascontiguousarray(byte.astype(np.uint8).reshape(k // 512, 16, n))


def unpack_fp4(words, scales):
    g, _, n = scales.shape
    words = np.ascontiguousarray(words).reshape(g, 128, n, 2)
    nib = np.empty((g, 128, n, 4), np.uint8)
    nib[..., 0::2] = words & 0xF
    nib[..., 1::2] = words >> 4
    vals = E2M1[nib] * np.repeat(np.exp2(scales.astype(np.float64) - 127.0), 8, axis=1)[..., None]
    return vals.transpose(0, 1, 3, 2).reshape(g * 512, n)


def sigmoid(v):
    return 1.0 / (1.0 + np.exp(-np.maximum(v, -700.0)))

def planes(y):
    n, m = y.shape
    v = y.astype(np.float32).astype(ml_dtypes.bfloat16).astype(np.float64).reshape(n // 32, 32, m)
    top = np.abs(v).max(1)
    byte = np.clip(np.where(top > 0, np.frexp(top)[1] - 1 + 127 - 7, 1), 1, 254)
    codes = (v * np.exp2(127.0 - byte)[:, None, :]).reshape(n, m).astype(np.float32).astype(ml_dtypes.float8_e4m3fn).view(np.uint8)
    words = codes.reshape(n // 512, 128, 4, m).transpose(0, 1, 3, 2)
    return np.ascontiguousarray(words), np.ascontiguousarray(byte.astype(np.uint8).reshape(n // 512, 16, m))


K, T, S, N, H = 512, 2048, 512, 512, 512


def setup_inputs():
    n = np.random.standard_normal
    s = mx_kscale(K)[:, None]
    u = mx_kscale(H)
    packed_xT = pack_weight(n((K, T)) * s)
    packed_w1 = pack_fp4(n((K, H)) / np.sqrt(K) / s)
    packed_w2 = pack_fp4(n((H, H)) / np.sqrt(H) / u[:, None])
    packed_w3 = pack_fp4(n((H, N)) / np.sqrt(H) / u[:, None])
    return {
        "x_words": packed_xT[0],
        "x_scales": packed_xT[1],
        "w1_words": packed_w1[0],
        "w1_scales": packed_w1[1],
        "gn": (np.random.uniform(0.5, 1.5, (H, 1)) * u[:, None]).astype(np.float32),
        "w2_words": packed_w2[0],
        "w2_scales": packed_w2[1],
        "res": n((N, S)).astype(np.float32),
        "w3_words": packed_w3[0],
        "w3_scales": packed_w3[1],
        "offs": striped(np.random.permutation(T)[:S]),
        "e1": striped8(np.stack([np.random.permutation(S) for _ in range(8)])),
        "e2": striped8(np.stack([np.random.permutation(S) for _ in range(8)])),
        "mv": striped8(np.stack([np.random.permutation(S) for _ in range(8)])),
    }


def reference(x_words, x_scales, w1_words, w1_scales, gn, w2_words, w2_scales, res, w3_words, w3_scales, offs, e1, e2, mv):
    xq = unpack_weight(x_words, x_scales)[:, unstriped(offs)]
    p = sigmoid(unpack_fp4(w1_words, w1_scales).T @ xq)
    a = p[np.arange(H)[:, None], runs(e1, H)]
    b = p[np.arange(H)[:, None], runs(e2, H)]
    ab = a * b
    z = f64(gn) * (ab / (ab + (-1.0 * a + 1) * (-1.0 * b + 1) + 0.05))
    h = np.tanh(unpack_fp4(w2_words, w2_scales).T @ mxq(z, 0, "e4m3"))
    z2 = f64(gn) * (h[np.arange(H)[:, None], runs(mv, H)])
    out_0 = f64(res) + (unpack_fp4(w3_words, w3_scales).T @ mxq(z2, 0, "e4m3"))
    return (out_0,) + planes(out_0)

@@ -1,0 +1,204 @@
+import math
+from contextlib import ExitStack
+
+import concourse.mybir as mybir
+
+K, T, S = 512, 2048, 512
+FLOPS = 3 * 2 * 512 * 512 * 512
+
+F32 = mybir.dt.float32
+BF16 = mybir.dt.bfloat16
+I32 = mybir.dt.int32
+U32 = mybir.dt.uint32
+U16 = mybir.dt.uint16
+U8 = mybir.dt.uint8
+FP8X4 = mybir.dt.float8_e4m3fn_x4
+FP4X4 = mybir.dt.float4_e2m1fn_x4
+ACT = mybir.ActivationFunctionType
+ALU = mybir.AluOpType
+
+P = 128
+PACK = 4
+X_FIRST = 768
+JOIN_CHUNKS = ((0, 256), (256, 512))
+OUT_CHUNKS = ((0, 256), (256, 384), (384, 512))
+
+
+def woven(tile):
+    return tile[:].rearrange("p (c i) t -> p c t i", i=4)
+
+
+def planar(tile):
+    return tile[:].rearrange("p t (c i) -> p c t i", i=4)
+
+
+def tile_picked_oddsjoin_none_po_kernel(
+    tc, x_words, x_scales, w1_words, w1_scales, gn, w2_words, w2_scales, res, w3_words, w3_scales,
+    offs, e1, e2, mv, out_0, out_1, out_2,
+):
+    nc = tc.nc
+    with ExitStack() as ctx:
+        lists = ctx.enter_context(tc.tile_pool(name="lists", bufs=1))
+        keep = ctx.enter_context(tc.tile_pool(name="keep", bufs=1))
+        psum = ctx.enter_context(tc.psum_pool(name="psum", bufs=1))
+
+        def load_list(src, name):
+            tile = lists.tile([P, S // 16], U16, name=name)
+            nc.sync.dma_start(tile[:], src)
+            return tile
+
+        def load_scale_rows(tile, src, queues):
+            for q in range(4):
+                queues[q].dma_start(tile[32 * q : 32 * q + 4, :].bitcast(I32), src[0, 4 * q : 4 * q + 4, :].bitcast(I32))
+
+        xs_all = keep.tile([P, T], U8, name="xs_all", align_bytes=64)
+        ws_raw = keep.tile([P, 512], U8, name="ws_raw", align_bytes=64)
+        ww_raw = keep.tile([P, 1024], U8, name="ww_raw", align_bytes=64)
+        nc.vector.memset(xs_all[:].bitcast(I32), 0)
+        nc.gpsimd.memset(ws_raw[:].bitcast(I32), 0)
+
+        xw_all = keep.tile([P, T], I32, name="xw_all", tag="wide", align_bytes=64)
+        offs_t = load_list(offs, "offs_t")
+        nc.sync.dma_start(ww_raw[:].bitcast(I32), w1_words[0].bitcast(I32))
+        x_rows = x_words[0].rearrange("p c r -> p (c r)").bitcast(I32)
+        nc.sync.dma_start(xw_all[:, :X_FIRST], x_rows[:, :X_FIRST])
+        load_scale_rows(xs_all, x_scales, [nc.sync] * 4)
+        nc.sync.dma_start(xw_all[:, X_FIRST:], x_rows[:, X_FIRST:])
+        load_scale_rows(ws_raw, w1_scales, [nc.sync] * 4)
+        e1_t = load_list(e1, "e1_t")
+        e2_t = load_list(e2, "e2_t")
+        gain = keep.tile([P, PACK], F32, name="gain")
+        nc.sync.dma_start(gain[:], gn.rearrange("(p t) o -> p (t o)", t=PACK))
+        mv_t = load_list(mv, "mv_t")
+
+        def deal(name, words_tag, scales_tag):
+            words = keep.tile([P, 1024], U8, name=name + "_words", tag=words_tag, align_bytes=64)
+            scales = keep.tile([P, 512], U8, name=name + "_scales", tag=scales_tag, align_bytes=64)
+            nc.vector.tensor_copy(
+                words[:].rearrange("p (t m b) -> p t m b", t=PACK, b=2),
+                ww_raw[:].rearrange("p (m t b) -> p t m b", t=PACK, b=2),
+            )
+            nc.vector.tensor_copy(
+                scales[:].rearrange("p (t m) -> p t m", t=PACK), ws_raw[:].rearrange("p (m t) -> p t m", t=PACK)
+            )
+            return words, scales
+
+        def load_weight(words, scales):
+            nc.sync.dma_start(ww_raw[:].bitcast(I32), words[0].bitcast(I32))
+            load_scale_rows(ws_raw, scales, [nc.sync] * 4)
+
+        def product(out, weight, t, codes, scales):
+            nc.tensor.matmul_mx(
+                out,
+                lhsT=weight[0][:, 256 * t : 256 * (t + 1)].bitcast(FP4X4),
+                lhsT_scale=weight[1][:, 128 * t : 128 * (t + 1)],
+                rhs=codes.bitcast(FP8X4),
+                rhs_scale=scales,
+                start=True,
+                stop=True,
+            )
+
+        w1 = deal("w1", "w1_words", "w1_scales")
+        load_weight(w2_words, w2_scales)
+
+        xs = keep.tile([P, S], U8, name="xs", align_bytes=64)
+        xw = keep.tile([P, S], I32, name="xw", align_bytes=64)
+        nc.vector.tensor_copy(xs[:], xs_all[:].indirect(offs_t[:]))
+        nc.vector.tensor_copy(xw[:].bitcast(U32), xw_all[:].bitcast(U32).indirect(offs_t[:]))
+
+        res_t = keep.tile([P, PACK, S], F32, name="res_t", tag="wide", align_bytes=64)
+        nc.sync.dma_start(res_t[:], res.rearrange("(p t) j -> p t j", t=PACK))
+
+        odds = []
+        for t in range(PACK):
+            bank = psum.tile([P, S], F32, name="first%d" % t, tag="a%d" % t)
+            product(bank[:], w1, t, xw[:], xs[:])
+            s_t = keep.tile([P, S], F32, name="odds%d" % t, align_bytes=64)
+            nc.scalar.activation(s_t[:], bank[:], ACT.Sigmoid, bias=-math.log(21.0), scale=1.0)
+            odds.append(s_t)
+
+        w2 = deal("w2", "w2_words", "w2_scales")
+        load_weight(w3_words, w3_scales)
+
+        z_codes = keep.tile([P, S], I32, name="z_codes", align_bytes=64)
+        z_scales = keep.tile([P, S], U8, name="z_scales", align_bytes=64)
+        second = {
+            (lo, u): psum.tile([P, 2, hi - lo], F32, name="second%d_%d" % (lo, u)) for lo, hi in JOIN_CHUNKS for u in (0, 1)
+        }
+        factors = []
+        for lo, hi in JOIN_CHUNKS:
+            n = hi - lo
+            entries = slice(lo // 16, hi // 16)
+            left = keep.tile([P, PACK, n], F32, name="left%d" % lo, align_bytes=64)
+            both = keep.tile([P, PACK, n], F32, name="both%d" % lo, align_bytes=64)
+            gained = keep.tile([P, PACK, n], F32, name="gained%d" % lo, align_bytes=64)
+            square = keep.tile([P, PACK, n], F32, name="square%d" % lo, align_bytes=64)
+            inverse = keep.tile([P, PACK, n], F32, name="inverse%d" % lo, align_bytes=64)
+            for pair in (0, 2):
+                for t in (pair, pair + 1):
+                    nc.vector.tensor_copy(left[:, t, :], odds[t][:].indirect(e1_t[:, entries]))
+                for t in (pair, pair + 1):
+                    nc.vector.tensor_tensor(both[:, t, :], odds[t][:].indirect(e2_t[:, entries]), left[:, t, :], ALU.mult)
+                two = slice(pair, pair + 2)
+                nc.scalar.activation(
+                    square[:, two, :], both[:, two, :], ACT.Square, bias=1.0 / 420.0, scale=440.0 / 420.0
+                )
+                nc.scalar.activation(inverse[:, two, :], square[:, two, :], ACT.Abs_reciprocal_sqrt)
+                for t in (pair, pair + 1):
+                    nc.scalar.activation(gained[:, t, :], both[:, t, :], ACT.Copy, scale=gain[:, t : t + 1])
+            factors.append((gained, inverse))
+        for (lo, hi), (gained, inverse) in zip(JOIN_CHUNKS, factors):
+            z = keep.tile([P, hi - lo, PACK], BF16, name="z%d" % lo, align_bytes=64)
+            nc.vector.tensor_tensor(woven(z), planar(gained), planar(inverse), ALU.mult)
+            nc.vector.quantize_mx(
+                out=z_codes[:, lo:hi].bitcast(FP8X4), scales=z_scales[:, lo:hi], in_=z[:].rearrange("p n t -> p (n t)")
+            )
+            for t in range(PACK):
+                product(second[lo, t // 2][:, t % 2, :], w2, t, z_codes[:, lo:hi], z_scales[:, lo:hi])
+
+        w3 = deal("w3", "z256", "gained256")
+
+        hidden = [keep.tile([P, S], F32, name="hidden%d" % t, align_bytes=64) for t in range(PACK)]
+        for lo, hi in JOIN_CHUNKS:
+            for t in range(PACK):
+                nc.scalar.activation(hidden[t][:, lo:hi], second[lo, t // 2][:, t % 2, :], ACT.Tanh)
+
+        y_codes = keep.tile([P, S], I32, name="y_codes", align_bytes=64)
+        y_scales = keep.tile([P, S], U8, name="y_scales", align_bytes=64)
+        out_rows = out_0.rearrange("(p t) j -> p t j", t=PACK)
+        out_words = out_1[0].rearrange("p c r -> p (c r)").bitcast(I32)
+        bank_number = 0
+        for lo, hi in OUT_CHUNKS:
+            n = hi - lo
+            entries = slice(lo // 16, hi // 16)
+            moved = keep.tile([P, PACK, n], F32, name="moved%d" % lo, align_bytes=64)
+            z2_rows = keep.tile([P, PACK, n], BF16, name="z2_rows%d" % lo, align_bytes=64)
+            z2 = keep.tile([P, n, PACK], BF16, name="z2_%d" % lo, align_bytes=64)
+            z2_codes = keep.tile([P, n], I32, name="z2_codes%d" % lo, align_bytes=64)
+            z2_scales = keep.tile([P, n], U8, name="z2_scales%d" % lo, align_bytes=64)
+            y = keep.tile([P, PACK, n], F32, name="y%d" % lo, align_bytes=64)
+            y16 = keep.tile([P, n, PACK], BF16, name="y16_%d" % lo, align_bytes=64)
+            for t in range(PACK):
+                nc.vector.tensor_copy(moved[:, t, :], hidden[t][:].indirect(mv_t[:, entries]))
+                nc.scalar.activation(z2_rows[:, t, :], moved[:, t, :], ACT.Copy, scale=gain[:, t : t + 1])
+            nc.vector.tensor_copy(woven(z2), planar(z2_rows))
+            nc.vector.quantize_mx(
+                out=z2_codes[:].bitcast(FP8X4), scales=z2_scales[:], in_=z2[:].rearrange("p n t -> p (n t)")
+            )
+            per_bank = 512 // n
+            for t0 in range(0, PACK, per_bank):
+                bank = psum.tile([P, per_bank, n], F32, name="third%d" % bank_number, tag="a%d" % bank_number)
+                bank_number = bank_number + 1
+                for u in range(per_bank):
+                    product(bank[:, u, :], w3, t0 + u, z2_codes[:], z2_scales[:])
+                rows = slice(t0, t0 + per_bank)
+                nc.vector.tensor_tensor(y[:, rows, :], bank[:], res_t[:, rows, lo:hi], ALU.add)
+            nc.sync.dma_start(out_rows[:, :, lo:hi], y[:])
+            nc.scalar.copy(woven(y16), planar(y))
+            nc.vector.quantize_mx(
+                out=y_codes[:, lo:hi].bitcast(FP8X4), scales=y_scales[:, lo:hi], in_=y16[:].rearrange("p n t -> p (n t)")
+            )
+            nc.sync.dma_start(out_words[:, lo:hi], y_codes[:, lo:hi])
+        for q in range(4):
+            queue = nc.sync if q % 2 == 0 else nc.scalar
+            queue.dma_start(out_2[0, 4 * q : 4 * q + 4, :].bitcast(I32), y_scales[32 * q : 32 * q + 4, :].bitcast(I32))

@@ -3,7 +3,6 @@ from contextlib import ExitStack
 
 import concourse.mybir as mybir
 
-K, T, S = 512, 2048, 512
 FLOPS = 3 * 2 * 512 * 512 * 512
 
 F32 = mybir.dt.float32
@@ -19,9 +18,15 @@ ALU = mybir.AluOpType
 
 P = 128
 PACK = 4
+T = 2048
+S = 512
+WIDTH = 512
+GROUP = 16
+HALVES = ((0, S // 2), (S // 2, S))
+CHUNK = 128
 X_FIRST = 768
-JOIN_CHUNKS = ((0, 256), (256, 512))
-OUT_CHUNKS = ((0, 256), (256, 384), (384, 512))
+SCALAR_E1_TILE = 3
+SCALAR_MV_TILE = 2
 
 
 def woven(tile):
@@ -32,6 +37,10 @@ def planar(tile):
     return tile[:].rearrange("p t (c i) -> p c t i", i=4)
 
 
+def entries(list_tile, lo, hi):
+    return list_tile[:, lo // GROUP : hi // GROUP]
+
+
 def tile_picked_oddsjoin_none_po_kernel(
     tc, x_words, x_scales, w1_words, w1_scales, gn, w2_words, w2_scales, res, w3_words, w3_scales,
     offs, e1, e2, mv, out_0, out_1, out_2,
@@ -40,165 +49,205 @@ def tile_picked_oddsjoin_none_po_kernel(
     with ExitStack() as ctx:
         lists = ctx.enter_context(tc.tile_pool(name="lists", bufs=1))
         keep = ctx.enter_context(tc.tile_pool(name="keep", bufs=1))
+        ring = ctx.enter_context(tc.tile_pool(name="ring", bufs=2))
         psum = ctx.enter_context(tc.psum_pool(name="psum", bufs=1))
 
+        def sbuf(shape, dtype, name, tag=None):
+            return keep.tile(shape, dtype, name=name, tag=tag or name, align_bytes=64)
+
+        def bank(shape, name, number):
+            return psum.tile(shape, F32, name=name, tag="bank%d" % number)
+
         def load_list(src, name):
-            tile = lists.tile([P, S // 16], U16, name=name)
+            tile = lists.tile([P, S // GROUP], U16, name=name)
             nc.sync.dma_start(tile[:], src)
             return tile
 
-        def load_scale_rows(tile, src, queues):
+        def load_scale_rows(tile, src):
             for q in range(4):
-                queues[q].dma_start(tile[32 * q : 32 * q + 4, :].bitcast(I32), src[0, 4 * q : 4 * q + 4, :].bitcast(I32))
+                nc.sync.dma_start(tile[32 * q : 32 * q + 4, :].bitcast(I32), src[0, 4 * q : 4 * q + 4, :].bitcast(I32))
 
-        xs_all = keep.tile([P, T], U8, name="xs_all", align_bytes=64)
-        ws_raw = keep.tile([P, 512], U8, name="ws_raw", align_bytes=64)
-        ww_raw = keep.tile([P, 1024], U8, name="ww_raw", align_bytes=64)
-        nc.vector.memset(xs_all[:].bitcast(I32), 0)
-        nc.gpsimd.memset(ws_raw[:].bitcast(I32), 0)
+        def load_words(src):
+            nc.sync.dma_start(raw_words[:].bitcast(I32), src[0].bitcast(I32))
 
-        xw_all = keep.tile([P, T], I32, name="xw_all", tag="wide", align_bytes=64)
-        offs_t = load_list(offs, "offs_t")
-        nc.sync.dma_start(ww_raw[:].bitcast(I32), w1_words[0].bitcast(I32))
-        x_rows = x_words[0].rearrange("p c r -> p (c r)").bitcast(I32)
-        nc.sync.dma_start(xw_all[:, :X_FIRST], x_rows[:, :X_FIRST])
-        load_scale_rows(xs_all, x_scales, [nc.sync] * 4)
-        nc.sync.dma_start(xw_all[:, X_FIRST:], x_rows[:, X_FIRST:])
-        load_scale_rows(ws_raw, w1_scales, [nc.sync] * 4)
-        e1_t = load_list(e1, "e1_t")
-        e2_t = load_list(e2, "e2_t")
-        gain = keep.tile([P, PACK], F32, name="gain")
-        nc.sync.dma_start(gain[:], gn.rearrange("(p t) o -> p (t o)", t=PACK))
-        mv_t = load_list(mv, "mv_t")
-
-        def deal(name, words_tag, scales_tag):
-            words = keep.tile([P, 1024], U8, name=name + "_words", tag=words_tag, align_bytes=64)
-            scales = keep.tile([P, 512], U8, name=name + "_scales", tag=scales_tag, align_bytes=64)
+        def deal_words(name, tag=None):
+            words = sbuf([P, 2 * WIDTH], U8, name, tag)
             nc.vector.tensor_copy(
                 words[:].rearrange("p (t m b) -> p t m b", t=PACK, b=2),
-                ww_raw[:].rearrange("p (m t b) -> p t m b", t=PACK, b=2),
+                raw_words[:].rearrange("p (m t b) -> p t m b", t=PACK, b=2),
             )
+            return words
+
+        def deal_scales(scales, tiles):
             nc.vector.tensor_copy(
-                scales[:].rearrange("p (t m) -> p t m", t=PACK), ws_raw[:].rearrange("p (m t) -> p t m", t=PACK)
+                scales[:].rearrange("p (t m) -> p t m", t=PACK)[:, tiles, :],
+                raw_scales[:].rearrange("p (m t) -> p t m", t=PACK)[:, tiles, :],
             )
-            return words, scales
 
-        def load_weight(words, scales):
-            nc.sync.dma_start(ww_raw[:].bitcast(I32), words[0].bitcast(I32))
-            load_scale_rows(ws_raw, scales, [nc.sync] * 4)
-
-        def product(out, weight, t, codes, scales):
+        def product(out, weight_words, weight_scales, t, codes, scales):
             nc.tensor.matmul_mx(
                 out,
-                lhsT=weight[0][:, 256 * t : 256 * (t + 1)].bitcast(FP4X4),
-                lhsT_scale=weight[1][:, 128 * t : 128 * (t + 1)],
+                lhsT=weight_words[:, 2 * P * t : 2 * P * (t + 1)].bitcast(FP4X4),
+                lhsT_scale=weight_scales[:, P * t : P * (t + 1)],
                 rhs=codes.bitcast(FP8X4),
                 rhs_scale=scales,
                 start=True,
                 stop=True,
             )
 
-        w1 = deal("w1", "w1_words", "w1_scales")
-        load_weight(w2_words, w2_scales)
+        def quantise(codes, scales, values):
+            nc.vector.quantize_mx(out=codes.bitcast(FP8X4), scales=scales, in_=values[:].rearrange("p n t -> p (n t)"))
 
-        xs = keep.tile([P, S], U8, name="xs", align_bytes=64)
-        xw = keep.tile([P, S], I32, name="xw", align_bytes=64)
-        nc.vector.tensor_copy(xs[:], xs_all[:].indirect(offs_t[:]))
-        nc.vector.tensor_copy(xw[:].bitcast(U32), xw_all[:].bitcast(U32).indirect(offs_t[:]))
+        x_scales_all = sbuf([P, T], U8, "x_scales_all")
+        raw_scales = sbuf([P, WIDTH], U8, "raw_scales")
+        raw_words = sbuf([P, 2 * WIDTH], U8, "raw_words")
+        nc.vector.memset(x_scales_all[:].bitcast(I32), 0)
+        nc.gpsimd.memset(raw_scales[:].bitcast(I32), 0)
 
-        res_t = keep.tile([P, PACK, S], F32, name="res_t", tag="wide", align_bytes=64)
-        nc.sync.dma_start(res_t[:], res.rearrange("(p t) j -> p t j", t=PACK))
+        x_words_all = sbuf([P, T], I32, "x_words_all")
+        offs_list = load_list(offs, "offs_list")
+        load_words(w1_words)
+        x_rows = x_words[0].rearrange("p c r -> p (c r)").bitcast(I32)
+        nc.sync.dma_start(x_words_all[:, :X_FIRST], x_rows[:, :X_FIRST])
+        load_scale_rows(x_scales_all, x_scales)
+        nc.sync.dma_start(x_words_all[:, X_FIRST:], x_rows[:, X_FIRST:])
+        load_scale_rows(raw_scales, w1_scales)
+        e1_list = load_list(e1, "e1_list")
+        e2_list = load_list(e2, "e2_list")
 
-        odds = []
-        for t in range(PACK):
-            bank = psum.tile([P, S], F32, name="first%d" % t, tag="a%d" % t)
-            product(bank[:], w1, t, xw[:], xs[:])
-            s_t = keep.tile([P, S], F32, name="odds%d" % t, align_bytes=64)
-            nc.scalar.activation(s_t[:], bank[:], ACT.Sigmoid, bias=-math.log(21.0), scale=1.0)
-            odds.append(s_t)
+        w1_codes = deal_words("w1_codes")
+        load_words(w2_words)
+        gain = keep.tile([P, PACK], F32, name="gain")
+        nc.sync.dma_start(gain[:], gn.rearrange("(p t) o -> p (t o)", t=PACK))
+        mv_list = load_list(mv, "mv_list")
+        twice_gain = keep.tile([P, PACK], F32, name="twice_gain")
+        minus_gain = keep.tile([P, PACK], F32, name="minus_gain")
+        nc.gpsimd.tensor_scalar(twice_gain[:], gain[:], 2.0, 0.0, ALU.mult, ALU.add)
+        nc.gpsimd.tensor_scalar(minus_gain[:], gain[:], -1.0, 0.0, ALU.mult, ALU.add)
 
-        w2 = deal("w2", "w2_words", "w2_scales")
-        load_weight(w3_words, w3_scales)
-
-        z_codes = keep.tile([P, S], I32, name="z_codes", align_bytes=64)
-        z_scales = keep.tile([P, S], U8, name="z_scales", align_bytes=64)
-        second = {
-            (lo, u): psum.tile([P, 2, hi - lo], F32, name="second%d_%d" % (lo, u)) for lo, hi in JOIN_CHUNKS for u in (0, 1)
-        }
-        factors = []
-        for lo, hi in JOIN_CHUNKS:
-            n = hi - lo
-            entries = slice(lo // 16, hi // 16)
-            left = keep.tile([P, PACK, n], F32, name="left%d" % lo, align_bytes=64)
-            both = keep.tile([P, PACK, n], F32, name="both%d" % lo, align_bytes=64)
-            gained = keep.tile([P, PACK, n], F32, name="gained%d" % lo, align_bytes=64)
-            square = keep.tile([P, PACK, n], F32, name="square%d" % lo, align_bytes=64)
-            inverse = keep.tile([P, PACK, n], F32, name="inverse%d" % lo, align_bytes=64)
-            for pair in (0, 2):
-                for t in (pair, pair + 1):
-                    nc.vector.tensor_copy(left[:, t, :], odds[t][:].indirect(e1_t[:, entries]))
-                for t in (pair, pair + 1):
-                    nc.vector.tensor_tensor(both[:, t, :], odds[t][:].indirect(e2_t[:, entries]), left[:, t, :], ALU.mult)
-                two = slice(pair, pair + 2)
-                nc.scalar.activation(
-                    square[:, two, :], both[:, two, :], ACT.Square, bias=1.0 / 420.0, scale=440.0 / 420.0
-                )
-                nc.scalar.activation(inverse[:, two, :], square[:, two, :], ACT.Abs_reciprocal_sqrt)
-                for t in (pair, pair + 1):
-                    nc.scalar.activation(gained[:, t, :], both[:, t, :], ACT.Copy, scale=gain[:, t : t + 1])
-            factors.append((gained, inverse))
-        for (lo, hi), (gained, inverse) in zip(JOIN_CHUNKS, factors):
-            z = keep.tile([P, hi - lo, PACK], BF16, name="z%d" % lo, align_bytes=64)
-            nc.vector.tensor_tensor(woven(z), planar(gained), planar(inverse), ALU.mult)
-            nc.vector.quantize_mx(
-                out=z_codes[:, lo:hi].bitcast(FP8X4), scales=z_scales[:, lo:hi], in_=z[:].rearrange("p n t -> p (n t)")
+        picked_scales = sbuf([P, S], U8, "picked_scales")
+        picked_words = sbuf([P, S], I32, "picked_words")
+        w1_bytes = sbuf([P, WIDTH], U8, "w1_bytes")
+        nc.vector.tensor_copy(picked_scales[:], x_scales_all[:].indirect(offs_list[:]))
+        for lo, hi in HALVES:
+            nc.vector.tensor_copy(
+                picked_words[:, lo:hi].bitcast(U32), x_words_all[:].bitcast(U32).indirect(entries(offs_list, lo, hi))
             )
+            if lo == 0:
+                deal_scales(w1_bytes, slice(0, 1))
+        deal_scales(w1_bytes, slice(1, PACK))
+        load_scale_rows(raw_scales, w2_scales)
+
+        residual = sbuf([P, PACK, S], F32, "residual", tag="x_words_all")
+        nc.sync.dma_start(residual[:], res.rearrange("(p t) j -> p t j", t=PACK))
+
+        shift = -math.log(21.0)
+        odds = []
+        logits = sbuf([P, S], F32, "logits")
+        for t in range(PACK):
+            odds.append(sbuf([P, S], F32, "odds%d" % t))
+            for lo, hi in HALVES if t == 0 else ((0, S),):
+                first = bank([P, hi - lo], "first%d_%d" % (t, lo), t if lo == 0 else 5)
+                product(first[:], w1_codes, w1_bytes, t, picked_words[:, lo:hi], picked_scales[:, lo:hi])
+                if t == SCALAR_E1_TILE:
+                    nc.scalar.activation(logits[:], first[:], ACT.Identity, bias=shift, scale=1.0)
+                nc.scalar.activation(odds[t][:, lo:hi], first[:], ACT.Sigmoid, bias=shift, scale=1.0)
+        left = [sbuf([P, PACK, hi - lo], F32, "left%d" % lo) for lo, hi in HALVES]
+        for h, (lo, hi) in enumerate(HALVES):
+            nc.scalar.activation(left[h][:, SCALAR_E1_TILE, :], logits[:].indirect(entries(e1_list, lo, hi)), ACT.Sigmoid)
+
+        w2_bytes = sbuf([P, WIDTH], U8, "w2_bytes")
+        w2_codes = deal_words("w2_codes")
+        load_words(w3_words)
+
+        z_codes = sbuf([P, S], I32, "z_codes")
+        z_scales = sbuf([P, S], U8, "z_scales")
+        factors = []
+        for h, (lo, hi) in enumerate(HALVES):
+            both = sbuf([P, PACK, hi - lo], F32, "both%d" % lo)
+            gained = sbuf([P, PACK, hi - lo], F32, "gained%d" % lo)
+            square = sbuf([P, PACK, hi - lo], F32, "square%d" % lo)
+            inverse = sbuf([P, PACK, hi - lo], F32, "inverse%d" % lo)
             for t in range(PACK):
-                product(second[lo, t // 2][:, t % 2, :], w2, t, z_codes[:, lo:hi], z_scales[:, lo:hi])
+                if t != SCALAR_E1_TILE:
+                    nc.vector.tensor_copy(left[h][:, t, :], odds[t][:].indirect(entries(e1_list, lo, hi)))
+                nc.vector.tensor_tensor(
+                    both[:, t, :], odds[t][:].indirect(entries(e2_list, lo, hi)), left[h][:, t, :], ALU.mult
+                )
+                nc.scalar.activation(square[:, t, :], both[:, t, :], ACT.Square, bias=1.0 / 420.0, scale=440.0 / 420.0)
+                if h == 0:
+                    nc.scalar.activation(gained[:, t, :], both[:, t, :], ACT.Copy, scale=gain[:, t : t + 1])
+                else:
+                    nc.vector.tensor_scalar(gained[:, t, :], both[:, t, :], gain[:, t : t + 1], None, ALU.mult)
+                nc.scalar.activation(inverse[:, t, :], square[:, t, :], ACT.Abs_reciprocal_sqrt)
+            factors.append((gained, inverse))
+        deal_scales(w2_bytes, slice(0, PACK))
+        load_scale_rows(raw_scales, w3_scales)
 
-        w3 = deal("w3", "z256", "gained256")
-
-        hidden = [keep.tile([P, S], F32, name="hidden%d" % t, align_bytes=64) for t in range(PACK)]
-        for lo, hi in JOIN_CHUNKS:
+        second = {}
+        for h, (lo, hi) in enumerate(HALVES):
+            gained, inverse = factors[h]
+            z = sbuf([P, hi - lo, PACK], BF16, "z%d" % lo)
+            nc.vector.tensor_tensor(woven(z), planar(gained), planar(inverse), ALU.mult)
+            quantise(z_codes[:, lo:hi], z_scales[:, lo:hi], z)
+            if h == 0:
+                pairs = [bank([P, 2, hi - lo], "second_pair%d" % u, 4 + u) for u in range(2)]
+                sums = [pairs[t // 2][:, t % 2, :] for t in range(PACK)]
+            else:
+                sums = [bank([P, hi - lo], "second_tile%d" % t, t)[:] for t in range(PACK)]
             for t in range(PACK):
-                nc.scalar.activation(hidden[t][:, lo:hi], second[lo, t // 2][:, t % 2, :], ACT.Tanh)
+                second[h, t] = sums[t]
+                product(sums[t], w2_codes, w2_bytes, t, z_codes[:, lo:hi], z_scales[:, lo:hi])
 
-        y_codes = keep.tile([P, S], I32, name="y_codes", align_bytes=64)
-        y_scales = keep.tile([P, S], U8, name="y_scales", align_bytes=64)
+        w3_bytes = sbuf([P, WIDTH], U8, "w3_bytes", tag="inverse%d" % HALVES[1][0])
+        deal_scales(w3_bytes, slice(0, PACK))
+        w3_codes = deal_words("w3_codes", tag="z%d" % HALVES[1][0])
+
+        hidden = [sbuf([P, S], F32, "hidden%d" % t) for t in range(PACK)]
+        for h, (lo, hi) in enumerate(HALVES):
+            for t in range(PACK):
+                func = ACT.Copy if t == SCALAR_MV_TILE else ACT.Sigmoid
+                nc.scalar.activation(hidden[t][:, lo:hi], second[h, t], func, scale=2.0)
+
+        y_codes = sbuf([P, S], I32, "y_codes")
+        y_scales = sbuf([P, S], U8, "y_scales")
         out_rows = out_0.rearrange("(p t) j -> p t j", t=PACK)
         out_words = out_1[0].rearrange("p c r -> p (c r)").bitcast(I32)
-        bank_number = 0
-        for lo, hi in OUT_CHUNKS:
-            n = hi - lo
-            entries = slice(lo // 16, hi // 16)
-            moved = keep.tile([P, PACK, n], F32, name="moved%d" % lo, align_bytes=64)
-            z2_rows = keep.tile([P, PACK, n], BF16, name="z2_rows%d" % lo, align_bytes=64)
-            z2 = keep.tile([P, n, PACK], BF16, name="z2_%d" % lo, align_bytes=64)
-            z2_codes = keep.tile([P, n], I32, name="z2_codes%d" % lo, align_bytes=64)
-            z2_scales = keep.tile([P, n], U8, name="z2_scales%d" % lo, align_bytes=64)
-            y = keep.tile([P, PACK, n], F32, name="y%d" % lo, align_bytes=64)
-            y16 = keep.tile([P, n, PACK], BF16, name="y16_%d" % lo, align_bytes=64)
+        vector_tiles = [t for t in range(PACK) if t != SCALAR_MV_TILE]
+        for c, lo in enumerate(range(0, S, CHUNK)):
+            hi = lo + CHUNK
+            fetched = sbuf([P, CHUNK], F32, "fetched%d" % c)
+            nc.scalar.activation(fetched[:], hidden[SCALAR_MV_TILE][:].indirect(entries(mv_list, lo, hi)), ACT.Sigmoid)
+            moved = ring.tile([P, len(vector_tiles), CHUNK], F32, name="moved", align_bytes=64)
+            z2_rows = sbuf([P, PACK, CHUNK], BF16, "z2_rows%d" % c)
+            z2 = sbuf([P, CHUNK, PACK], BF16, "z2_%d" % c)
+            z2_codes = sbuf([P, CHUNK], I32, "z2_codes%d" % c)
+            z2_scales = sbuf([P, CHUNK], U8, "z2_scales%d" % c)
+            y = sbuf([P, PACK, CHUNK], F32, "y%d" % c)
+            y_rounded = sbuf([P, CHUNK, PACK], BF16, "y_rounded%d" % c)
             for t in range(PACK):
-                nc.vector.tensor_copy(moved[:, t, :], hidden[t][:].indirect(mv_t[:, entries]))
-                nc.scalar.activation(z2_rows[:, t, :], moved[:, t, :], ACT.Copy, scale=gain[:, t : t + 1])
+                if t == SCALAR_MV_TILE:
+                    row = fetched[:]
+                else:
+                    row = moved[:, vector_tiles.index(t), :]
+                    nc.vector.tensor_copy(row, hidden[t][:].indirect(entries(mv_list, lo, hi)))
+                nc.scalar.activation(
+                    z2_rows[:, t, :], row, ACT.Identity, scale=twice_gain[:, t : t + 1], bias=minus_gain[:, t : t + 1]
+                )
             nc.vector.tensor_copy(woven(z2), planar(z2_rows))
-            nc.vector.quantize_mx(
-                out=z2_codes[:].bitcast(FP8X4), scales=z2_scales[:], in_=z2[:].rearrange("p n t -> p (n t)")
-            )
-            per_bank = 512 // n
-            for t0 in range(0, PACK, per_bank):
-                bank = psum.tile([P, per_bank, n], F32, name="third%d" % bank_number, tag="a%d" % bank_number)
-                bank_number = bank_number + 1
-                for u in range(per_bank):
-                    product(bank[:, u, :], w3, t0 + u, z2_codes[:], z2_scales[:])
-                rows = slice(t0, t0 + per_bank)
-                nc.vector.tensor_tensor(y[:, rows, :], bank[:], res_t[:, rows, lo:hi], ALU.add)
+            quantise(z2_codes[:], z2_scales[:], z2)
+            third = bank([P, PACK, CHUNK], "third%d" % c, (6, 7, 4, 5)[c])
+            for t in range(PACK):
+                product(third[:, t, :], w3_codes, w3_bytes, t, z2_codes[:], z2_scales[:])
+            nc.vector.tensor_tensor(y[:], third[:], residual[:, :, lo:hi], ALU.add)
             nc.sync.dma_start(out_rows[:, :, lo:hi], y[:])
-            nc.scalar.copy(woven(y16), planar(y))
-            nc.vector.quantize_mx(
-                out=y_codes[:, lo:hi].bitcast(FP8X4), scales=y_scales[:, lo:hi], in_=y16[:].rearrange("p n t -> p (n t)")
-            )
+            if hi < S:
+                nc.scalar.copy(woven(y_rounded), planar(y))
+            else:
+                nc.vector.tensor_copy(woven(y_rounded), planar(y))
+            quantise(y_codes[:, lo:hi], y_scales[:, lo:hi], y_rounded)
             nc.sync.dma_start(out_words[:, lo:hi], y_codes[:, lo:hi])
+
         for q in range(4):
             queue = nc.sync if q % 2 == 0 else nc.scalar
             queue.dma_start(out_2[0, 4 * q : 4 * q + 4, :].bitcast(I32), y_scales[32 * q : 32 * q + 4, :].bitcast(I32))

@@ -224,7 +224,6 @@ def tile_picked_oddsjoin_none_po_kernel(
             z2_codes = sbuf([P, CHUNK], I32, "z2_codes%d" % c)
             z2_scales = sbuf([P, CHUNK], U8, "z2_scales%d" % c)
             y = sbuf([P, PACK, CHUNK], F32, "y%d" % c)
-            y_rounded = sbuf([P, CHUNK, PACK], BF16, "y_rounded%d" % c)
             for t in range(PACK):
                 if t == SCALAR_MV_TILE:
                     row = fetched[:]
@@ -234,18 +233,28 @@ def tile_picked_oddsjoin_none_po_kernel(
                 nc.scalar.activation(
                     z2_rows[:, t, :], row, ACT.Identity, scale=twice_gain[:, t : t + 1], bias=minus_gain[:, t : t + 1]
                 )
-            nc.vector.tensor_copy(woven(z2), planar(z2_rows))
+            if hi < S:
+                nc.gpsimd.tensor_scalar(z2[:], z2_rows[:].rearrange("p t n -> p n t"), 1.0, 0.0, ALU.mult, ALU.add)
+            else:
+                nc.vector.tensor_copy(woven(z2), planar(z2_rows))
             quantise(z2_codes[:], z2_scales[:], z2)
             third = bank([P, PACK, CHUNK], "third%d" % c, (6, 7, 4, 5)[c])
             for t in range(PACK):
                 product(third[:, t, :], w3_codes, w3_bytes, t, z2_codes[:], z2_scales[:])
-            nc.vector.tensor_tensor(y[:], third[:], residual[:, :, lo:hi], ALU.add)
+            pieces = ((0, CHUNK),) if hi < S else ((0, CHUNK // 2), (CHUNK // 2, CHUNK))
+            for start, stop in pieces:
+                nc.vector.tensor_tensor(
+                    y[:, :, start:stop], third[:, :, start:stop], residual[:, :, lo + start : lo + stop], ALU.add
+                )
             nc.sync.dma_start(out_rows[:, :, lo:hi], y[:])
-            if hi < S:
-                nc.scalar.copy(woven(y_rounded), planar(y))
-            else:
-                nc.vector.tensor_copy(woven(y_rounded), planar(y))
-            quantise(y_codes[:, lo:hi], y_scales[:, lo:hi], y_rounded)
+            for start, stop in pieces:
+                y_rounded = sbuf([P, stop - start, PACK], BF16, "y_rounded%d_%d" % (c, start))
+                values = y[:, :, start:stop].rearrange("p t (c i) -> p c t i", i=4)
+                if hi < S:
+                    nc.scalar.copy(woven(y_rounded), values)
+                else:
+                    nc.vector.tensor_copy(woven(y_rounded), values)
+                quantise(y_codes[:, lo + start : lo + stop], y_scales[:, lo + start : lo + stop], y_rounded)
             nc.sync.dma_start(out_words[:, lo:hi], y_codes[:, lo:hi])
 
         for q in range(4):

import math
from contextlib import ExitStack

import concourse.mybir as mybir

FLOPS = 3 * 2 * 512 * 512 * 512

F32 = mybir.dt.float32
BF16 = mybir.dt.bfloat16
I32 = mybir.dt.int32
U32 = mybir.dt.uint32
U16 = mybir.dt.uint16
U8 = mybir.dt.uint8
FP8X4 = mybir.dt.float8_e4m3fn_x4
FP4X4 = mybir.dt.float4_e2m1fn_x4
ACT = mybir.ActivationFunctionType
ALU = mybir.AluOpType

P = 128
PACK = 4
T = 2048
S = 512
WIDTH = 512
GROUP = 16
HALVES = ((0, S // 2), (S // 2, S))
CHUNK = 128
X_FIRST = 768
SCALAR_E1_TILE = 3
SCALAR_MV_TILE = 2


def woven(tile):
    return tile[:].rearrange("p (c i) t -> p c t i", i=4)


def planar(tile):
    return tile[:].rearrange("p t (c i) -> p c t i", i=4)


def entries(list_tile, lo, hi):
    return list_tile[:, lo // GROUP : hi // GROUP]


def tile_picked_oddsjoin_none_po_kernel(
    tc, x_words, x_scales, w1_words, w1_scales, gn, w2_words, w2_scales, res, w3_words, w3_scales,
    offs, e1, e2, mv, out_0, out_1, out_2,
):
    nc = tc.nc
    with ExitStack() as ctx:
        lists = ctx.enter_context(tc.tile_pool(name="lists", bufs=1))
        keep = ctx.enter_context(tc.tile_pool(name="keep", bufs=1))
        ring = ctx.enter_context(tc.tile_pool(name="ring", bufs=2))
        psum = ctx.enter_context(tc.psum_pool(name="psum", bufs=1))

        def sbuf(shape, dtype, name, tag=None):
            return keep.tile(shape, dtype, name=name, tag=tag or name, align_bytes=64)

        def bank(shape, name, number):
            return psum.tile(shape, F32, name=name, tag="bank%d" % number)

        def load_list(src, name):
            tile = lists.tile([P, S // GROUP], U16, name=name)
            nc.sync.dma_start(tile[:], src)
            return tile

        def load_scale_rows(tile, src):
            for q in range(4):
                nc.sync.dma_start(tile[32 * q : 32 * q + 4, :].bitcast(I32), src[0, 4 * q : 4 * q + 4, :].bitcast(I32))

        def load_words(src):
            nc.sync.dma_start(raw_words[:].bitcast(I32), src[0].bitcast(I32))

        def deal_words(name, tag=None):
            words = sbuf([P, 2 * WIDTH], U8, name, tag)
            nc.vector.tensor_copy(
                words[:].rearrange("p (t m b) -> p t m b", t=PACK, b=2),
                raw_words[:].rearrange("p (m t b) -> p t m b", t=PACK, b=2),
            )
            return words

        def deal_scales(scales, tiles):
            nc.vector.tensor_copy(
                scales[:].rearrange("p (t m) -> p t m", t=PACK)[:, tiles, :],
                raw_scales[:].rearrange("p (m t) -> p t m", t=PACK)[:, tiles, :],
            )

        def product(out, weight_words, weight_scales, t, codes, scales):
            nc.tensor.matmul_mx(
                out,
                lhsT=weight_words[:, 2 * P * t : 2 * P * (t + 1)].bitcast(FP4X4),
                lhsT_scale=weight_scales[:, P * t : P * (t + 1)],
                rhs=codes.bitcast(FP8X4),
                rhs_scale=scales,
                start=True,
                stop=True,
            )

        def quantise(codes, scales, values):
            nc.vector.quantize_mx(out=codes.bitcast(FP8X4), scales=scales, in_=values[:].rearrange("p n t -> p (n t)"))

        x_scales_all = sbuf([P, T], U8, "x_scales_all")
        raw_scales = sbuf([P, WIDTH], U8, "raw_scales")
        raw_words = sbuf([P, 2 * WIDTH], U8, "raw_words")
        nc.vector.memset(x_scales_all[:].bitcast(I32), 0)
        nc.gpsimd.memset(raw_scales[:].bitcast(I32), 0)

        x_words_all = sbuf([P, T], I32, "x_words_all")
        offs_list = load_list(offs, "offs_list")
        load_words(w1_words)
        x_rows = x_words[0].rearrange("p c r -> p (c r)").bitcast(I32)
        nc.sync.dma_start(x_words_all[:, :X_FIRST], x_rows[:, :X_FIRST])
        load_scale_rows(x_scales_all, x_scales)
        nc.sync.dma_start(x_words_all[:, X_FIRST:], x_rows[:, X_FIRST:])
        load_scale_rows(raw_scales, w1_scales)
        e1_list = load_list(e1, "e1_list")
        e2_list = load_list(e2, "e2_list")

        w1_codes = deal_words("w1_codes")
        load_words(w2_words)
        gain = keep.tile([P, PACK], F32, name="gain")
        nc.sync.dma_start(gain[:], gn.rearrange("(p t) o -> p (t o)", t=PACK))
        mv_list = load_list(mv, "mv_list")
        twice_gain = keep.tile([P, PACK], F32, name="twice_gain")
        minus_gain = keep.tile([P, PACK], F32, name="minus_gain")
        nc.gpsimd.tensor_scalar(twice_gain[:], gain[:], 2.0, 0.0, ALU.mult, ALU.add)
        nc.gpsimd.tensor_scalar(minus_gain[:], gain[:], -1.0, 0.0, ALU.mult, ALU.add)

        picked_scales = sbuf([P, S], U8, "picked_scales")
        picked_words = sbuf([P, S], I32, "picked_words")
        w1_bytes = sbuf([P, WIDTH], U8, "w1_bytes")
        nc.vector.tensor_copy(picked_scales[:], x_scales_all[:].indirect(offs_list[:]))
        for lo, hi in HALVES:
            nc.vector.tensor_copy(
                picked_words[:, lo:hi].bitcast(U32), x_words_all[:].bitcast(U32).indirect(entries(offs_list, lo, hi))
            )
            if lo == 0:
                deal_scales(w1_bytes, slice(0, 1))
        deal_scales(w1_bytes, slice(1, PACK))
        load_scale_rows(raw_scales, w2_scales)

        residual = sbuf([P, PACK, S], F32, "residual", tag="x_words_all")
        nc.sync.dma_start(residual[:], res.rearrange("(p t) j -> p t j", t=PACK))

        shift = -math.log(21.0)
        odds = []
        logits = sbuf([P, S], F32, "logits")
        for t in range(PACK):
            odds.append(sbuf([P, S], F32, "odds%d" % t))
            for lo, hi in HALVES if t == 0 else ((0, S),):
                first = bank([P, hi - lo], "first%d_%d" % (t, lo), t if lo == 0 else 5)
                product(first[:], w1_codes, w1_bytes, t, picked_words[:, lo:hi], picked_scales[:, lo:hi])
                if t == SCALAR_E1_TILE:
                    nc.scalar.activation(logits[:], first[:], ACT.Identity, bias=shift, scale=1.0)
                nc.scalar.activation(odds[t][:, lo:hi], first[:], ACT.Sigmoid, bias=shift, scale=1.0)
        left = [sbuf([P, PACK, hi - lo], F32, "left%d" % lo) for lo, hi in HALVES]
        for h, (lo, hi) in enumerate(HALVES):
            nc.scalar.activation(left[h][:, SCALAR_E1_TILE, :], logits[:].indirect(entries(e1_list, lo, hi)), ACT.Sigmoid)

        w2_bytes = sbuf([P, WIDTH], U8, "w2_bytes")
        w2_codes = deal_words("w2_codes")
        load_words(w3_words)

        z_codes = sbuf([P, S], I32, "z_codes")
        z_scales = sbuf([P, S], U8, "z_scales")
        factors = []
        for h, (lo, hi) in enumerate(HALVES):
            both = sbuf([P, PACK, hi - lo], F32, "both%d" % lo)
            gained = sbuf([P, PACK, hi - lo], F32, "gained%d" % lo)
            square = sbuf([P, PACK, hi - lo], F32, "square%d" % lo)
            inverse = sbuf([P, PACK, hi - lo], F32, "inverse%d" % lo)
            for t in range(PACK):
                if t != SCALAR_E1_TILE:
                    nc.vector.tensor_copy(left[h][:, t, :], odds[t][:].indirect(entries(e1_list, lo, hi)))
                nc.vector.tensor_tensor(
                    both[:, t, :], odds[t][:].indirect(entries(e2_list, lo, hi)), left[h][:, t, :], ALU.mult
                )
                nc.scalar.activation(square[:, t, :], both[:, t, :], ACT.Square, bias=1.0 / 420.0, scale=440.0 / 420.0)
                if h == 0:
                    nc.scalar.activation(gained[:, t, :], both[:, t, :], ACT.Copy, scale=gain[:, t : t + 1])
                else:
                    nc.vector.tensor_scalar(gained[:, t, :], both[:, t, :], gain[:, t : t + 1], None, ALU.mult)
                nc.scalar.activation(inverse[:, t, :], square[:, t, :], ACT.Abs_reciprocal_sqrt)
            factors.append((gained, inverse))
        deal_scales(w2_bytes, slice(0, PACK))
        load_scale_rows(raw_scales, w3_scales)

        second = {}
        for h, (lo, hi) in enumerate(HALVES):
            gained, inverse = factors[h]
            z = sbuf([P, hi - lo, PACK], BF16, "z%d" % lo)
            nc.vector.tensor_tensor(woven(z), planar(gained), planar(inverse), ALU.mult)
            quantise(z_codes[:, lo:hi], z_scales[:, lo:hi], z)
            if h == 0:
                pairs = [bank([P, 2, hi - lo], "second_pair%d" % u, 4 + u) for u in range(2)]
                sums = [pairs[t // 2][:, t % 2, :] for t in range(PACK)]
            else:
                sums = [bank([P, hi - lo], "second_tile%d" % t, t)[:] for t in range(PACK)]
            for t in range(PACK):
                second[h, t] = sums[t]
                product(sums[t], w2_codes, w2_bytes, t, z_codes[:, lo:hi], z_scales[:, lo:hi])

        w3_bytes = sbuf([P, WIDTH], U8, "w3_bytes", tag="inverse%d" % HALVES[1][0])
        deal_scales(w3_bytes, slice(0, PACK))
        w3_codes = deal_words("w3_codes", tag="z%d" % HALVES[1][0])

        hidden = [sbuf([P, S], F32, "hidden%d" % t) for t in range(PACK)]
        for h, (lo, hi) in enumerate(HALVES):
            for t in range(PACK):
                func = ACT.Copy if t == SCALAR_MV_TILE else ACT.Sigmoid
                nc.scalar.activation(hidden[t][:, lo:hi], second[h, t], func, scale=2.0)

        y_codes = sbuf([P, S], I32, "y_codes")
        y_scales = sbuf([P, S], U8, "y_scales")
        out_rows = out_0.rearrange("(p t) j -> p t j", t=PACK)
        out_words = out_1[0].rearrange("p c r -> p (c r)").bitcast(I32)
        vector_tiles = [t for t in range(PACK) if t != SCALAR_MV_TILE]
        for c, lo in enumerate(range(0, S, CHUNK)):
            hi = lo + CHUNK
            fetched = sbuf([P, CHUNK], F32, "fetched%d" % c)
            nc.scalar.activation(fetched[:], hidden[SCALAR_MV_TILE][:].indirect(entries(mv_list, lo, hi)), ACT.Sigmoid)
            moved = ring.tile([P, len(vector_tiles), CHUNK], F32, name="moved", align_bytes=64)
            z2_rows = sbuf([P, PACK, CHUNK], BF16, "z2_rows%d" % c)
            z2 = sbuf([P, CHUNK, PACK], BF16, "z2_%d" % c)
            z2_codes = sbuf([P, CHUNK], I32, "z2_codes%d" % c)
            z2_scales = sbuf([P, CHUNK], U8, "z2_scales%d" % c)
            y = sbuf([P, PACK, CHUNK], F32, "y%d" % c)
            for t in range(PACK):
                if t == SCALAR_MV_TILE:
                    row = fetched[:]
                else:
                    row = moved[:, vector_tiles.index(t), :]
                    nc.vector.tensor_copy(row, hidden[t][:].indirect(entries(mv_list, lo, hi)))
                nc.scalar.activation(
                    z2_rows[:, t, :], row, ACT.Identity, scale=twice_gain[:, t : t + 1], bias=minus_gain[:, t : t + 1]
                )
            if hi < S:
                nc.gpsimd.tensor_scalar(z2[:], z2_rows[:].rearrange("p t n -> p n t"), 1.0, 0.0, ALU.mult, ALU.add)
            else:
                nc.vector.tensor_copy(woven(z2), planar(z2_rows))
            quantise(z2_codes[:], z2_scales[:], z2)
            third = bank([P, PACK, CHUNK], "third%d" % c, (6, 7, 4, 5)[c])
            for t in range(PACK):
                product(third[:, t, :], w3_codes, w3_bytes, t, z2_codes[:], z2_scales[:])
            pieces = ((0, CHUNK),) if hi < S else ((0, CHUNK // 2), (CHUNK // 2, CHUNK))
            for start, stop in pieces:
                nc.vector.tensor_tensor(
                    y[:, :, start:stop], third[:, :, start:stop], residual[:, :, lo + start : lo + stop], ALU.add
                )
            nc.sync.dma_start(out_rows[:, :, lo:hi], y[:])
            for start, stop in pieces:
                y_rounded = sbuf([P, stop - start, PACK], BF16, "y_rounded%d_%d" % (c, start))
                values = y[:, :, start:stop].rearrange("p t (c i) -> p c t i", i=4)
                if hi < S:
                    nc.scalar.copy(woven(y_rounded), values)
                else:
                    nc.vector.tensor_copy(woven(y_rounded), values)
                quantise(y_codes[:, lo + start : lo + stop], y_scales[:, lo + start : lo + stop], y_rounded)
            nc.sync.dma_start(out_words[:, lo:hi], y_codes[:, lo:hi])

        for q in range(4):
            queue = nc.sync if q % 2 == 0 else nc.scalar
            queue.dma_start(out_2[0, 4 * q : 4 * q + 4, :].bitcast(I32), y_scales[32 * q : 32 * q + 4, :].bitcast(I32))
